import numpy as np
import ml_dtypes


def mxq(x, axis, fmt="e4m3"):
    dtype, down = {"e4m3": (ml_dtypes.float8_e4m3fn, 7), "e5m2": (ml_dtypes.float8_e5m2, 14)}[fmt]
    v = np.moveaxis(np.asarray(x, np.float32).astype(ml_dtypes.bfloat16).astype(np.float64), axis, -1)
    blocks = v.reshape(v.shape[:-1] + (-1, 32))
    amax = np.abs(blocks).max(-1, keepdims=True)
    byte = np.maximum(np.where(amax > 0, np.frexp(amax)[1] - 1 + 127, 0) - down, 1)
    scale = np.exp2(byte - 127.0)
    codes = (blocks / scale).astype(np.float32).astype(dtype).astype(np.float64)
    return np.moveaxis((codes * scale).reshape(v.shape), -1, axis)


WIDE = False


def mx_kscale(k):
    if not WIDE:
        return np.ones(k)
    levels = np.array([10, -10, 5, -5, 0])
    if k % 512:
        return np.exp2(np.random.permutation(np.resize(levels, k // 32))).repeat(32)
    a = np.empty((k // 512, 16))
    for p in range(k // 512):
        a[p, :8] = np.random.permutation(np.resize(levels, 8))
        for g in range(8):
            far = levels[np.abs(levels - a[p, g]) >= 10]
            a[p, g + 8] = far[np.random.randint(len(far))]
    return np.exp2(a.ravel()).repeat(32)


def f64(x):
    return np.asarray(x).astype(np.float64)


def striped(idx):
    return np.tile(idx.reshape(-1, 16).T, (8, 1)).astype(np.uint16)


def unstriped(offs):
    return offs[:16].T.reshape(-1).astype(np.int64)


E2M1 = np.array([0.0, 0.5, 1.0, 1.5, 2.0, 3.0, 4.0, 6.0, -0.0, -0.5, -1.0, -1.5, -2.0, -3.0, -4.0, -6.0])


def pack_weight(w, fmt):
    k, n = w.shape
    w = f64(np.asarray(w, np.float32).astype(ml_dtypes.bfloat16)).reshape(k // 32, 32, n)
    amax = np.abs(w).max(1)
    if fmt == "e4m3":
        byte = np.frexp(amax)[1] - 1 + 127 - 7
    else:
        mant, ex = np.frexp(amax / 6.0)
        byte = np.where(mant > 0.5, ex, ex - 1) + 127
    byte = np.clip(np.where(amax > 0, byte, 1), 1, 254)
    scaled = (w * np.exp2(127.0 - byte)[:, None, :]).reshape(k, n).astype(np.float32)
    by_word = np.ascontiguousarray(scaled.reshape(k // 512, 128, 4, n).transpose(0, 1, 3, 2))
    if fmt == "e4m3":
        words = by_word.astype(ml_dtypes.float8_e4m3fn).view(np.uint8)
    else:
        c = by_word.astype(ml_dtypes.float4_e2m1fn).view(np.uint8) & 0xF
        words = (c[..., 0::2] | (c[..., 1::2] << 4)).reshape(k // 512, 128, 2 * n)
    return np.ascontiguousarray(words), np.ascontiguousarray(byte.astype(np.uint8).reshape(k // 512, 16, n))


def unpack_weight(words, scales, fmt):
    g, _, n = scales.shape
    words = np.ascontiguousarray(words).reshape(g, 128, n, -1)
    if fmt == "e4m3":
        vals = words.view(ml_dtypes.float8_e4m3fn).astype(np.float64)
    else:
        nib = np.empty((g, 128, n, 4), np.uint8)
        nib[..., 0::2] = words & 0xF
        nib[..., 1::2] = words >> 4
        vals = E2M1[nib]
    vals = vals * np.repeat(np.exp2(scales.astype(np.float64) - 127.0), 8, axis=1)[..., None]
    return vals.transpose(0, 1, 3, 2).reshape(g * 512, n)


def gelu(v):
    return 0.5 * v * (1.0 + np.tanh(np.sqrt(2.0 / np.pi) * (v + 0.044715 * v**3)))


def bf(x):
    return np.asarray(x, np.float32).astype(ml_dtypes.bfloat16)


def planes(Y):
    n, m = Y.shape
    b = f64(bf(Y)).reshape(n // 32, 32, m)
    amax = np.abs(b).max(1)
    byte = np.clip(np.where(amax > 0, np.frexp(amax)[1] - 1 + 127 - 7, 1), 1, 254)
    codes = (b * np.exp2(127.0 - byte)[:, None, :]).reshape(n, m).astype(np.float32).astype(ml_dtypes.float8_e4m3fn).view(np.uint8)
    words = codes.reshape(n // 512, 128, 4, m).transpose(0, 1, 3, 2)
    return np.ascontiguousarray(words), np.ascontiguousarray(byte.astype(np.uint8).reshape(n // 512, 16, m))


K, T, S, H, N, P = 1536, 2048, 1024, 1024, 1024, 512


def setup_inputs():
    n = np.random.standard_normal
    s = mx_kscale(K)[:, None]
    u = mx_kscale(H)[:, None]
    tab_words, tab_scales = pack_weight(n((K, T)) * s, "e4m3")
    w4_words, w4_scales = pack_weight(0.8 * n((H, N)) / np.sqrt(H) / u, "e2m1")
    return {
        "tab_words": tab_words, "tab_scales": tab_scales,
        "offs": striped(np.random.permutation(T)[:S]),
        "pos1": striped(np.random.permutation(S)[:P]),
        "pos2": striped(np.random.permutation(S)[:P]),
        "w1": (0.9 * n((K, H)) / np.sqrt(K) / s).astype(np.float32),
        "temp": np.random.uniform(0.4, 1.6, H).astype(np.float32),
        "thr": n(H).astype(np.float32),
        "load": (5.0 * n((H, P)) * u).astype(np.float32),
        "cap": (0.5 * n(H) * u[:, 0]).astype(np.float32),
        "lean": (1.6 * n(H) * u[:, 0]).astype(np.float32),
        "w4_words": w4_words, "w4_scales": w4_scales,
        "rate": np.exp(0.8 * n(N)).astype(np.float32),
    }


def reference(tab_words, tab_scales, offs, pos1, pos2, w1, temp, thr, load, cap, lean,
              w4_words, w4_scales, rate):
    v = unpack_weight(tab_words, tab_scales, "e4m3")[:, unstriped(offs)]
    h = mxq(f64(w1), 0, "e4m3").T @ v
    top = h.max(axis=1)
    a = np.exp(f64(temp)[:, None] * (h[:, unstriped(pos1)] - top[:, None]))
    c = 1.0 / (1.0 + np.exp(-(h[:, unstriped(pos2)] + f64(thr)[:, None])))
    low = np.minimum(f64(load) * a, f64(cap)[:, None])
    z = low + c * f64(lean)[:, None]
    zq = mxq(z, 0, "e4m3")
    w4 = unpack_weight(w4_words, w4_scales, "e2m1")
    y = f64(rate)[:, None] * (w4.T @ zq)
    words, scales = planes(y)
    return y, words, scales

@@ -1,0 +1,283 @@
+from contextlib import ExitStack
+
+import concourse.mybir as mybir
+
+K, T, S, H, N, M = 1536, 2048, 1024, 1024, 1024, 512
+FLOPS = 2 * K * H * S + 2 * H * N * M
+
+F32 = mybir.dt.float32
+BF16 = mybir.dt.bfloat16
+I32 = mybir.dt.int32
+U32 = mybir.dt.uint32
+U16 = mybir.dt.uint16
+U8 = mybir.dt.uint8
+FP8X4 = mybir.dt.float8_e4m3fn_x4
+FP4X4 = mybir.dt.float4_e2m1fn_x4
+ALU = mybir.AluOpType
+ACT = mybir.ActivationFunctionType
+
+P = 128
+PACK = 4
+PASS = P * PACK
+KP = K // PASS
+HB = H // PASS
+NG = N // PASS
+BANK = 512
+SH = S // BANK
+MH = 2
+MW = M // MH
+LIST = 16
+
+
+def tile_list_covenant_watch_looks_kernel(
+    tc, tab_words, tab_scales, offs, pos1, pos2, w1, temp, thr, load, cap, lean, w4_words, w4_scales, rate, out_0, out_1, out_2
+):
+    nc = tc.nc
+    with ExitStack() as ctx:
+        keep = ctx.enter_context(tc.tile_pool(name="keep", bufs=1))
+        big = ctx.enter_context(tc.tile_pool(name="big", bufs=HB * KP))
+        stage = ctx.enter_context(tc.tile_pool(name="stage", bufs=3))
+        psum = ctx.enter_context(tc.psum_pool(name="psum", bufs=1))
+
+        def kept(shape, dtype, name, tag=None):
+            return keep.tile(shape, dtype, name=name, tag=tag or name, align_bytes=64)
+
+        offs_sb = kept([P, S // LIST], U16, "offs_sb")
+        pos1_sb = kept([P, M // LIST], U16, "pos1_sb")
+        pos2_sb = kept([P, M // LIST], U16, "pos2_sb")
+        tabw = [kept([P, T], U32, "tabw%d" % a) for a in range(KP)]
+        tabs = kept([P, T], U8, "tabs")
+        w1_raw = {}
+
+        def load_tab(a):
+            nc.sync.dma_start(out=tabw[a][:].bitcast(I32), in_=tab_words[a].rearrange("p t i -> p (t i)").bitcast(I32))
+
+        def load_w1(b, a):
+            w1_raw[b, a] = big.tile([P, PACK, PASS], F32, name="w1_raw", tag="big", align_bytes=64)
+            rows = w1[a * PASS : (a + 1) * PASS, b * PASS : (b + 1) * PASS]
+            nc.sync.dma_start(out=w1_raw[b, a][:], in_=rows.rearrange("(p j) c -> p j c", j=PACK))
+
+        rowvec = {}
+
+        def load_rowvec(name, vec):
+            rowvec[name] = kept([P, HB * PACK], F32, name + "_sb")
+            nc.sync.dma_start(
+                out=rowvec[name][:].rearrange("p (b t) -> p b t", t=PACK),
+                in_=vec.rearrange("(b p t) -> p b t", p=P, t=PACK),
+            )
+
+        w4s_raw = kept([P, HB, N], U8, "w4s_raw")
+        nc.vector.memset(tabs[:].bitcast(I32), 0)
+        nc.gpsimd.memset(w4s_raw[:].bitcast(I32), 0)
+        nc.sync.dma_start(offs_sb[:], offs)
+        for q in range(4):
+            nc.scalar.dma_start(
+                out=tabs[32 * q : 32 * q + 4 * KP, :].bitcast(I32),
+                in_=tab_scales[:, 4 * q : 4 * q + 4, :].bitcast(I32),
+            )
+        load_tab(0)
+        load_w1(0, 0)
+        load_w1(0, 1)
+        for q in range(4):
+            nc.scalar.dma_start(
+                out=w4s_raw[32 * q : 32 * q + 4, :, :].bitcast(I32),
+                in_=w4_scales[:, 4 * q : 4 * q + 4, :].rearrange("a r c -> r a c").bitcast(I32),
+            )
+        load_tab(1)
+        load_w1(0, 2)
+        load_tab(2)
+        load_rowvec("temp", temp)
+        nc.sync.dma_start(pos1_sb[:], pos1)
+        for a in range(KP):
+            load_w1(1, a)
+        load_sb = [kept([P, PACK, M], F32, "load_sb%d" % b) for b in range(HB)]
+        w4w_raw = kept([P, HB, 2 * N], U8, "w4w_raw")
+
+        def load_load(b):
+            nc.sync.dma_start(out=load_sb[b][:], in_=load[b * PASS : (b + 1) * PASS, :].rearrange("(p t) m -> p t m", t=PACK))
+
+        load_load(0)
+        nc.sync.dma_start(out=w4w_raw[:].bitcast(I32), in_=w4_words.rearrange("a p c -> p a c").bitcast(I32))
+        load_load(1)
+        load_rowvec("cap", cap)
+        nc.sync.dma_start(pos2_sb[:], pos2)
+        for name, vec in (("thr", thr), ("lean", lean), ("rate", rate)):
+            load_rowvec(name, vec)
+
+        def col(name, i):
+            return rowvec[name][:, i : i + 1]
+
+        vw = {(a, s): kept([P, BANK], U32, "vw%d_%d" % (a, s)) for a in range(KP) for s in range(SH)}
+        vs = [kept([P, BANK], U8, "vs%d" % s) for s in range(SH)]
+        w1q = {(b, a): kept([P, PASS], U32, "w1q%d_%d" % (b, a)) for b in range(HB) for a in range(KP)}
+        w1s = {(b, a): kept([P, PASS], U8, "w1s%d_%d" % (b, a)) for b in range(HB) for a in range(KP)}
+        acc = {}
+
+        def offs_slice(s):
+            return offs_sb[:, s * BANK // LIST : (s + 1) * BANK // LIST]
+
+        def gather_words(a, s):
+            nc.vector.tensor_copy(vw[a, s][:], tabw[a][:].indirect(offs_slice(s)))
+
+        def gather_scales(s):
+            nc.vector.tensor_copy(vs[s][:], tabs[:].indirect(offs_slice(s)))
+
+        def quantise_w1(b, a):
+            grouped = stage.tile([P, PASS * PACK], BF16, name="w1_bf", align_bytes=64)
+            nc.scalar.copy(
+                out=grouped[:].rearrange("p (t q j) -> p q j t", t=PACK, j=PACK),
+                in_=w1_raw[b, a][:].rearrange("p j (q t) -> p q j t", t=PACK),
+            )
+            nc.vector.quantize_mx(out=w1q[b, a][:].bitcast(FP8X4), scales=w1s[b, a][:], in_=grouped[:])
+
+        def first_pass(b, a):
+            for t in range(PACK):
+                for s in range(SH):
+                    if a == 0:
+                        acc[b, t, s] = psum.tile([P, BANK], F32, name="acc", tag="bank%d" % (t * SH + s))
+                    cols = slice(t * P, (t + 1) * P)
+                    nc.tensor.matmul_mx(
+                        out=acc[b, t, s][:],
+                        lhsT=w1q[b, a][:, cols].bitcast(FP8X4),
+                        lhsT_scale=w1s[b, a][:, cols],
+                        rhs=vw[a, s][:].bitcast(FP8X4),
+                        rhs_scale=vs[s][4 * a :, :],
+                        start=(a == 0),
+                        stop=(a == KP - 1),
+                    )
+
+        neg_temp = kept([P, HB * PACK], F32, "neg_temp")
+        w4s = kept([P, HB * N], U8, "w4s")
+        for a in range(KP):
+            for s in range(SH):
+                gather_words(a, s)
+            if a == 0:
+                for s in range(SH):
+                    gather_scales(s)
+            quantise_w1(0, a)
+            first_pass(0, a)
+            if a == 1:
+                nc.vector.tensor_copy(
+                    out=w4s[:].rearrange("p (g t q) -> p g t q", t=PACK, q=P),
+                    in_=w4s_raw[:].rearrange("p a (g q t) -> p (a g) t q", t=PACK, q=P),
+                )
+
+        nc.vector.tensor_scalar(neg_temp[:], rowvec["temp"][:], -1.0, None, ALU.mult)
+        h = [kept([P, S], F32, "h%d" % i) for i in range(HB * PACK)]
+        half_top = kept([P, HB * PACK * SH], F32, "half_top")
+        exp_bias = kept([P, HB * PACK], F32, "exp_bias", tag="after_exp")
+        low = [kept([P, M], F32, "low%d" % i) for i in range(HB * PACK)]
+
+        def leave_psum(b, t):
+            i = b * PACK + t
+            for s in range(SH):
+                nc.vector.tensor_scalar(
+                    h[i][:, s * BANK : (s + 1) * BANK], acc[b, t, s][:], 1.0, None, ALU.mult, ALU.max,
+                    accum_out=half_top[:, SH * i + s : SH * i + s + 1],
+                )
+            nc.vector.scalar_tensor_tensor(
+                exp_bias[:, i : i + 1], half_top[:, SH * i : SH * i + 1], half_top[:, SH * i + 1 : SH * i + 2],
+                neg_temp[:, i : i + 1], ALU.max, ALU.mult,
+            )
+
+        def look_exp(b, t):
+            i = b * PACK + t
+            nc.scalar.activation(
+                out=low[i][:], in_=h[i][:].indirect(pos1_sb[:]), func=ACT.Exp, bias=exp_bias[:, i : i + 1], scale=col("temp", i)
+            )
+
+        def make_low(b, t):
+            i = b * PACK + t
+            nc.vector.tensor_tensor(low[i][:], low[i][:], load_sb[b][:, t, :], ALU.mult)
+
+        def cap_low(b, t):
+            i = b * PACK + t
+            nc.vector.tensor_scalar(low[i][:], low[i][:], col("cap", i), None, ALU.min)
+
+        for t in range(PACK):
+            if t < KP:
+                quantise_w1(1, t)
+            leave_psum(0, t)
+            look_exp(0, t)
+        for a in range(KP):
+            first_pass(1, a)
+        w4w = kept([P, HB * 2 * N], U8, "w4w")
+        nc.vector.tensor_copy(
+            out=w4w[:].bitcast(U16).rearrange("p (g t q) -> p g t q", t=PACK, q=P),
+            in_=w4w_raw[:].bitcast(U16).rearrange("p a (g q t) -> p (a g) t q", t=PACK, q=P),
+        )
+        for t in range(PACK):
+            leave_psum(1, t)
+            look_exp(1, t)
+        for b in range(HB):
+            for t in range(PACK):
+                make_low(b, t)
+                if t > 0:
+                    cap_low(b, t - 1)
+            cap_low(b, PACK - 1)
+
+        z = kept([P, MH * HB * PACK * MW], F32, "z", tag="after_exp")
+        zq = {(u, b): kept([P, MW], U32, "zq%d_%d" % (u, b)) for u in range(MH) for b in range(HB)}
+        zs = {(u, b): kept([P, MW], U8, "zs%d_%d" % (u, b)) for u in range(MH) for b in range(HB)}
+        yq = {(u, g): kept([P, MW], U32, "yq%d_%d" % (u, g)) for u in range(MH) for g in range(NG)}
+        ys = kept([P, NG * M], U8, "ys")
+
+        def interleave(dst, src):
+            nc.vector.tensor_copy(
+                out=dst.rearrange("p (c i t) -> p c t i", i=PACK, t=PACK),
+                in_=src.rearrange("p (t c i) -> p c t i", i=PACK, t=PACK),
+            )
+
+        for u in range(MH):
+            mcols = slice(u * MW, (u + 1) * MW)
+            yacc = [psum.tile([P, MW], F32, name="yacc", tag="bank%d" % j) for j in range(NG * PACK)]
+            for b in range(HB):
+                base = (u * HB + b) * PACK * MW
+                for t in range(PACK):
+                    i = b * PACK + t
+                    zt = z[:, base + t * MW : base + (t + 1) * MW]
+                    nc.scalar.activation(
+                        out=zt, in_=h[i][:].indirect(pos2_sb[:, u * MW // LIST : (u + 1) * MW // LIST]),
+                        func=ACT.Sigmoid, bias=col("thr", i),
+                    )
+                    nc.vector.scalar_tensor_tensor(zt, zt, col("lean", i), low[i][:, mcols], ALU.mult, ALU.add)
+                z_bf = stage.tile([P, PACK * MW], BF16, name="z_bf", align_bytes=64)
+                interleave(z_bf[:], z[:, base : base + PACK * MW])
+                nc.vector.quantize_mx(out=zq[u, b][:].bitcast(FP8X4), scales=zs[u, b][:], in_=z_bf[:])
+                for j in range(NG * PACK):
+                    c0 = b * N + j * P
+                    nc.tensor.matmul_mx(
+                        out=yacc[j][:],
+                        lhsT=w4w[:, 2 * c0 : 2 * (c0 + P)].bitcast(FP4X4),
+                        lhsT_scale=w4s[:, c0 : c0 + P],
+                        rhs=zq[u, b][:].bitcast(FP8X4),
+                        rhs_scale=zs[u, b][:],
+                        start=(b == 0),
+                        stop=(b == HB - 1),
+                    )
+            for g in range(NG):
+                y = big.tile([P, PACK * MW], F32, name="y", tag="big", align_bytes=64)
+                for t in range(PACK):
+                    j = g * PACK + t
+                    yt = y[:, t * MW : (t + 1) * MW]
+                    if u == MH - 1 and t % 2 == 1:
+                        nc.vector.tensor_scalar(yt, yacc[j][:], col("rate", j), None, ALU.mult)
+                    else:
+                        nc.scalar.activation(out=yt, in_=yacc[j][:], func=ACT.Copy, scale=col("rate", j))
+                nc.sync.dma_start(
+                    out=out_0[g * PASS : (g + 1) * PASS, mcols].rearrange("(p t) m -> p t m", t=PACK),
+                    in_=y[:].rearrange("p (t m) -> p t m", t=PACK),
+                )
+                y_bf = stage.tile([P, PACK * MW], BF16, name="y_bf", align_bytes=64)
+                interleave(y_bf[:], y[:])
+                nc.vector.quantize_mx(
+                    out=yq[u, g][:].bitcast(FP8X4), scales=ys[:, g * M + u * MW : g * M + (u + 1) * MW], in_=y_bf[:]
+                )
+                nc.sync.dma_start(
+                    out=out_1[g].rearrange("p m t -> p (m t)").bitcast(I32)[:, mcols], in_=yq[u, g][:].bitcast(I32)
+                )
+        for q in range(4):
+            nc.scalar.dma_start(
+                out=out_2[:, 4 * q : 4 * q + 4, :].rearrange("g r m -> r g m").bitcast(I32),
+                in_=ys[32 * q : 32 * q + 4, :].bitcast(I32).rearrange("p (g m) -> p g m", g=NG),
+            )

@@ -19,14 +19,19 @@ ACT = mybir.ActivationFunctionType
 P = 128
 PACK = 4
 PASS = P * PACK
-KP = K // PASS
-HB = H // PASS
-NG = N // PASS
+QUADS, QUAD = 4, 32
 BANK = 512
-SH = S // BANK
-MH = 2
-MW = M // MH
 LIST = 16
+K_PASSES = K // PASS
+R_BLOCKS = H // PASS
+N_GROUPS = N // PASS
+ROW_TILES = R_BLOCKS * PACK
+S_HALVES = S // BANK
+M_HALVES = 2
+MW = M // M_HALVES
+TILE_PAIR = PACK // 2
+GPSIMD_TILES = 3
+FLOAT32_LOWEST = -3.4028234663852886e38
 
 
 def tile_list_covenant_watch_looks_kernel(
@@ -35,8 +40,8 @@ def tile_list_covenant_watch_looks_kernel(
     nc = tc.nc
     with ExitStack() as ctx:
         keep = ctx.enter_context(tc.tile_pool(name="keep", bufs=1))
-        big = ctx.enter_context(tc.tile_pool(name="big", bufs=HB * KP))
-        stage = ctx.enter_context(tc.tile_pool(name="stage", bufs=3))
+        big = ctx.enter_context(tc.tile_pool(name="big", bufs=5))
+        stage = ctx.enter_context(tc.tile_pool(name="stage", bufs=2))
         psum = ctx.enter_context(tc.psum_pool(name="psum", bufs=1))
 
         def kept(shape, dtype, name, tag=None):
@@ -45,239 +50,270 @@ def tile_list_covenant_watch_looks_kernel(
         offs_sb = kept([P, S // LIST], U16, "offs_sb")
         pos1_sb = kept([P, M // LIST], U16, "pos1_sb")
         pos2_sb = kept([P, M // LIST], U16, "pos2_sb")
-        tabw = [kept([P, T], U32, "tabw%d" % a) for a in range(KP)]
-        tabs = kept([P, T], U8, "tabs")
+        tab_w = [kept([P, T], U32, "tab_w%d" % a) for a in range(K_PASSES)]
+        tab_s = kept([P, T], U8, "tab_s")
+        w4_w_raw = kept([P, R_BLOCKS, 2 * N], U8, "w4_w_raw")
+        w4_s_raw = kept([P, R_BLOCKS, N], U8, "w4_s_raw")
+        load_sb = [kept([P, PACK, M], F32, "load_sb%d" % b) for b in range(R_BLOCKS)]
         w1_raw = {}
+        row_vec = {}
 
-        def load_tab(a):
-            nc.sync.dma_start(out=tabw[a][:].bitcast(I32), in_=tab_words[a].rearrange("p t i -> p (t i)").bitcast(I32))
+        def load_tab_words(a):
+            nc.sync.dma_start(out=tab_w[a][:].bitcast(I32), in_=tab_words[a].rearrange("p t i -> p (t i)").bitcast(I32))
 
         def load_w1(b, a):
             w1_raw[b, a] = big.tile([P, PACK, PASS], F32, name="w1_raw", tag="big", align_bytes=64)
             rows = w1[a * PASS : (a + 1) * PASS, b * PASS : (b + 1) * PASS]
             nc.sync.dma_start(out=w1_raw[b, a][:], in_=rows.rearrange("(p j) c -> p j c", j=PACK))
 
-        rowvec = {}
-
-        def load_rowvec(name, vec):
-            rowvec[name] = kept([P, HB * PACK], F32, name + "_sb")
+        def load_row_vec(name, vec):
+            row_vec[name] = kept([P, ROW_TILES], F32, name + "_sb")
             nc.sync.dma_start(
-                out=rowvec[name][:].rearrange("p (b t) -> p b t", t=PACK),
+                out=row_vec[name][:].rearrange("p (b t) -> p b t", t=PACK),
                 in_=vec.rearrange("(b p t) -> p b t", p=P, t=PACK),
             )
 
-        w4s_raw = kept([P, HB, N], U8, "w4s_raw")
-        nc.vector.memset(tabs[:].bitcast(I32), 0)
-        nc.gpsimd.memset(w4s_raw[:].bitcast(I32), 0)
+        def col(name, i):
+            return row_vec[name][:, i : i + 1]
+
+        nc.vector.memset(tab_s[:].bitcast(I32), 0)
+        nc.gpsimd.memset(w4_s_raw[:].bitcast(I32), 0)
+
+        load_tab_words(0)
         nc.sync.dma_start(offs_sb[:], offs)
-        for q in range(4):
-            nc.scalar.dma_start(
-                out=tabs[32 * q : 32 * q + 4 * KP, :].bitcast(I32),
-                in_=tab_scales[:, 4 * q : 4 * q + 4, :].bitcast(I32),
+        load_tab_words(1)
+        for q in range(QUADS):
+            nc.sync.dma_start(
+                out=tab_s[QUAD * q : QUAD * q + PACK * K_PASSES, :].bitcast(I32),
+                in_=tab_scales[:, PACK * q : PACK * (q + 1), :].bitcast(I32),
             )
-        load_tab(0)
         load_w1(0, 0)
         load_w1(0, 1)
-        for q in range(4):
-            nc.scalar.dma_start(
-                out=w4s_raw[32 * q : 32 * q + 4, :, :].bitcast(I32),
-                in_=w4_scales[:, 4 * q : 4 * q + 4, :].rearrange("a r c -> r a c").bitcast(I32),
+        for q in range(QUADS):
+            nc.sync.dma_start(
+                out=w4_s_raw[QUAD * q : QUAD * q + PACK, :, :].bitcast(I32),
+                in_=w4_scales[:, PACK * q : PACK * (q + 1), :].rearrange("a r c -> r a c").bitcast(I32),
             )
-        load_tab(1)
+        load_tab_words(2)
+        load_row_vec("temp", temp)
         load_w1(0, 2)
-        load_tab(2)
-        load_rowvec("temp", temp)
         nc.sync.dma_start(pos1_sb[:], pos1)
-        for a in range(KP):
+        for a in range(K_PASSES):
             load_w1(1, a)
-        load_sb = [kept([P, PACK, M], F32, "load_sb%d" % b) for b in range(HB)]
-        w4w_raw = kept([P, HB, 2 * N], U8, "w4w_raw")
-
-        def load_load(b):
-            nc.sync.dma_start(out=load_sb[b][:], in_=load[b * PASS : (b + 1) * PASS, :].rearrange("(p t) m -> p t m", t=PACK))
-
-        load_load(0)
-        nc.sync.dma_start(out=w4w_raw[:].bitcast(I32), in_=w4_words.rearrange("a p c -> p a c").bitcast(I32))
-        load_load(1)
-        load_rowvec("cap", cap)
+        load_row_vec("cap", cap)
+        for b in range(R_BLOCKS):
+            rows = load[b * PASS : (b + 1) * PASS, :]
+            nc.sync.dma_start(out=load_sb[b][:], in_=rows.rearrange("(p t) m -> p t m", t=PACK))
+        nc.sync.dma_start(out=w4_w_raw[:].bitcast(I32), in_=w4_words.rearrange("a p c -> p a c").bitcast(I32))
         nc.sync.dma_start(pos2_sb[:], pos2)
         for name, vec in (("thr", thr), ("lean", lean), ("rate", rate)):
-            load_rowvec(name, vec)
+            load_row_vec(name, vec)
 
-        def col(name, i):
-            return rowvec[name][:, i : i + 1]
+        v_w = {(a, s): kept([P, BANK], U32, "v_w%d_%d" % (a, s)) for a in range(K_PASSES) for s in range(S_HALVES)}
+        v_s = [kept([P, BANK], U8, "v_s%d" % s) for s in range(S_HALVES)]
+        w1_q = {(b, a): kept([P, PASS], U32, "w1_q%d_%d" % (b, a)) for b in range(R_BLOCKS) for a in range(K_PASSES)}
+        w1_s = {(b, a): kept([P, PASS], U8, "w1_s%d_%d" % (b, a)) for b in range(R_BLOCKS) for a in range(K_PASSES)}
+        h_acc = {}
 
-        vw = {(a, s): kept([P, BANK], U32, "vw%d_%d" % (a, s)) for a in range(KP) for s in range(SH)}
-        vs = [kept([P, BANK], U8, "vs%d" % s) for s in range(SH)]
-        w1q = {(b, a): kept([P, PASS], U32, "w1q%d_%d" % (b, a)) for b in range(HB) for a in range(KP)}
-        w1s = {(b, a): kept([P, PASS], U8, "w1s%d_%d" % (b, a)) for b in range(HB) for a in range(KP)}
-        acc = {}
-
-        def offs_slice(s):
+        def offs_half(s):
             return offs_sb[:, s * BANK // LIST : (s + 1) * BANK // LIST]
 
-        def gather_words(a, s):
-            nc.vector.tensor_copy(vw[a, s][:], tabw[a][:].indirect(offs_slice(s)))
+        def gather_words(a):
+            for s in range(S_HALVES):
+                nc.vector.tensor_copy(v_w[a, s][:], tab_w[a][:].indirect(offs_half(s)))
 
-        def gather_scales(s):
-            nc.vector.tensor_copy(vs[s][:], tabs[:].indirect(offs_slice(s)))
+        def gather_scales():
+            for s in range(S_HALVES):
+                nc.vector.tensor_copy(v_s[s][:], tab_s[:].indirect(offs_half(s)))
 
         def quantise_w1(b, a):
-            grouped = stage.tile([P, PASS * PACK], BF16, name="w1_bf", align_bytes=64)
-            nc.scalar.copy(
-                out=grouped[:].rearrange("p (t q j) -> p q j t", t=PACK, j=PACK),
-                in_=w1_raw[b, a][:].rearrange("p j (q t) -> p q j t", t=PACK),
-            )
-            nc.vector.quantize_mx(out=w1q[b, a][:].bitcast(FP8X4), scales=w1s[b, a][:], in_=grouped[:])
+            if (b, a) == (R_BLOCKS - 1, K_PASSES - 1):
+                w1_bf = kept([P, PASS * PACK], BF16, "w1_bf_last", tag="after_w1")
+            else:
+                w1_bf = stage.tile([P, PASS * PACK], BF16, name="w1_bf", bufs=3, align_bytes=64)
+            dst = w1_bf[:].rearrange("p (t q j) -> p q j t", t=PACK, j=PACK)
+            src = w1_raw[b, a][:].rearrange("p j (q t) -> p q j t", t=PACK)
+            if a == K_PASSES - 1:
+                shares = ((nc.vector.tensor_copy, 0, TILE_PAIR), (nc.scalar.copy, TILE_PAIR, PACK))
+            else:
+                shares = ((nc.scalar.copy, 0, PACK),)
+            for copy, t0, t1 in shares:
+                copy(out=dst[:, :, :, t0:t1], in_=src[:, :, :, t0:t1])
+                cols = slice(t0 * P, t1 * P)
+                nc.vector.quantize_mx(
+                    out=w1_q[b, a][:, cols].bitcast(FP8X4),
+                    scales=w1_s[b, a][:, cols],
+                    in_=w1_bf[:, t0 * PASS : t1 * PASS],
+                )
 
-        def first_pass(b, a):
-            for t in range(PACK):
-                for s in range(SH):
+        def first_product(b, t):
+            cols = slice(t * P, (t + 1) * P)
+            for a in range(K_PASSES):
+                for s in range(S_HALVES):
                     if a == 0:
-                        acc[b, t, s] = psum.tile([P, BANK], F32, name="acc", tag="bank%d" % (t * SH + s))
-                    cols = slice(t * P, (t + 1) * P)
+                        h_acc[b * PACK + t, s] = psum.tile([P, BANK], F32, name="h_acc", tag="bank%d" % (t * S_HALVES + s))
                     nc.tensor.matmul_mx(
-                        out=acc[b, t, s][:],
-                        lhsT=w1q[b, a][:, cols].bitcast(FP8X4),
-                        lhsT_scale=w1s[b, a][:, cols],
-                        rhs=vw[a, s][:].bitcast(FP8X4),
-                        rhs_scale=vs[s][4 * a :, :],
+                        out=h_acc[b * PACK + t, s][:],
+                        lhsT=w1_q[b, a][:, cols].bitcast(FP8X4),
+                        lhsT_scale=w1_s[b, a][:, cols],
+                        rhs=v_w[a, s][:].bitcast(FP8X4),
+                        rhs_scale=v_s[s][PACK * a :, :],
                         start=(a == 0),
-                        stop=(a == KP - 1),
+                        stop=(a == K_PASSES - 1),
                     )
 
-        neg_temp = kept([P, HB * PACK], F32, "neg_temp")
-        w4s = kept([P, HB * N], U8, "w4s")
-        for a in range(KP):
-            for s in range(SH):
-                gather_words(a, s)
-            if a == 0:
-                for s in range(SH):
-                    gather_scales(s)
-            quantise_w1(0, a)
-            first_pass(0, a)
-            if a == 1:
-                nc.vector.tensor_copy(
-                    out=w4s[:].rearrange("p (g t q) -> p g t q", t=PACK, q=P),
-                    in_=w4s_raw[:].rearrange("p a (g q t) -> p (a g) t q", t=PACK, q=P),
-                )
+        neg_temp = kept([P, ROW_TILES], F32, "neg_temp", tag="after_bias_a")
+        half_top = kept([P, S_HALVES, ROW_TILES], F32, "half_top", tag="after_bias_b")
+        exp_bias = kept([P, ROW_TILES], F32, "exp_bias", tag="after_exp")
+        h = [kept([P, S], F32, "h%d" % i) for i in range(ROW_TILES)]
+        look_a = [kept([P, M], F32, "look_a%d" % i) for i in range(ROW_TILES)]
 
-        nc.vector.tensor_scalar(neg_temp[:], rowvec["temp"][:], -1.0, None, ALU.mult)
-        h = [kept([P, S], F32, "h%d" % i) for i in range(HB * PACK)]
-        half_top = kept([P, HB * PACK * SH], F32, "half_top")
-        exp_bias = kept([P, HB * PACK], F32, "exp_bias", tag="after_exp")
-        low = [kept([P, M], F32, "low%d" % i) for i in range(HB * PACK)]
-
-        def leave_psum(b, t):
-            i = b * PACK + t
-            for s in range(SH):
+        def leave_psum(i):
+            for s in range(S_HALVES):
                 nc.vector.tensor_scalar(
-                    h[i][:, s * BANK : (s + 1) * BANK], acc[b, t, s][:], 1.0, None, ALU.mult, ALU.max,
-                    accum_out=half_top[:, SH * i + s : SH * i + s + 1],
+                    h[i][:, s * BANK : (s + 1) * BANK], h_acc[i, s][:], 1.0, None, ALU.mult, ALU.max,
+                    accum_out=half_top[:, s, i : i + 1],
                 )
-            nc.vector.scalar_tensor_tensor(
-                exp_bias[:, i : i + 1], half_top[:, SH * i : SH * i + 1], half_top[:, SH * i + 1 : SH * i + 2],
-                neg_temp[:, i : i + 1], ALU.max, ALU.mult,
+            nc.vector.tensor_scalar(
+                exp_bias[:, i : i + 1], half_top[:, 0, i : i + 1], half_top[:, 1, i : i + 1], neg_temp[:, i : i + 1],
+                ALU.max, ALU.mult,
             )
 
-        def look_exp(b, t):
-            i = b * PACK + t
+        def look_exp(i):
             nc.scalar.activation(
-                out=low[i][:], in_=h[i][:].indirect(pos1_sb[:]), func=ACT.Exp, bias=exp_bias[:, i : i + 1], scale=col("temp", i)
+                out=look_a[i][:], in_=h[i][:].indirect(pos1_sb[:]), func=ACT.Exp,
+                bias=exp_bias[:, i : i + 1], scale=col("temp", i),
             )
 
-        def make_low(b, t):
-            i = b * PACK + t
-            nc.vector.tensor_tensor(low[i][:], low[i][:], load_sb[b][:, t, :], ALU.mult)
-
-        def cap_low(b, t):
-            i = b * PACK + t
-            nc.vector.tensor_scalar(low[i][:], low[i][:], col("cap", i), None, ALU.min)
-
-        for t in range(PACK):
-            if t < KP:
-                quantise_w1(1, t)
-            leave_psum(0, t)
-            look_exp(0, t)
-        for a in range(KP):
-            first_pass(1, a)
-        w4w = kept([P, HB * 2 * N], U8, "w4w")
+        for a in range(K_PASSES - 1):
+            gather_words(a)
+        gather_scales()
+        for a in range(K_PASSES - 1):
+            quantise_w1(0, a)
+        gather_words(K_PASSES - 1)
+        quantise_w1(0, K_PASSES - 1)
+        nc.vector.tensor_scalar(neg_temp[:], row_vec["temp"][:], -1.0, None, ALU.mult)
+        w4_s = kept([P, R_BLOCKS * N], U8, "w4_s")
         nc.vector.tensor_copy(
-            out=w4w[:].bitcast(U16).rearrange("p (g t q) -> p g t q", t=PACK, q=P),
-            in_=w4w_raw[:].bitcast(U16).rearrange("p a (g q t) -> p (a g) t q", t=PACK, q=P),
+            out=w4_s[:].rearrange("p (g t q) -> p g t q", t=PACK, q=P),
+            in_=w4_s_raw[:].rearrange("p a (g q t) -> p (a g) t q", t=PACK, q=P),
         )
         for t in range(PACK):
-            leave_psum(1, t)
-            look_exp(1, t)
-        for b in range(HB):
-            for t in range(PACK):
-                make_low(b, t)
-                if t > 0:
-                    cap_low(b, t - 1)
-            cap_low(b, PACK - 1)
+            first_product(0, t)
+        for a in range(K_PASSES):
+            quantise_w1(1, a)
+        for t in range(PACK):
+            leave_psum(t)
+        for t in range(PACK):
+            look_exp(t)
+        for t in range(PACK):
+            first_product(1, t)
+        for t in range(PACK):
+            leave_psum(PACK + t)
+            look_exp(PACK + t)
 
-        z = kept([P, MH * HB * PACK * MW], F32, "z", tag="after_exp")
-        zq = {(u, b): kept([P, MW], U32, "zq%d_%d" % (u, b)) for u in range(MH) for b in range(HB)}
-        zs = {(u, b): kept([P, MW], U8, "zs%d_%d" % (u, b)) for u in range(MH) for b in range(HB)}
-        yq = {(u, g): kept([P, MW], U32, "yq%d_%d" % (u, g)) for u in range(MH) for g in range(NG)}
-        ys = kept([P, NG * M], U8, "ys")
+        w4_w = kept([P, R_BLOCKS * 2 * N], U8, "w4_w", tag="after_bias_b")
+        nc.vector.tensor_copy(
+            out=w4_w[:].bitcast(U16).rearrange("p (g t q) -> p g t q", t=PACK, q=P),
+            in_=w4_w_raw[:].bitcast(U16).rearrange("p a (g q t) -> p (a g) t q", t=PACK, q=P),
+        )
 
-        def interleave(dst, src):
+        low_gpsimd = kept([P, GPSIMD_TILES, M], F32, "low_gpsimd", tag="after_w1")
+        low_vector = kept([P, ROW_TILES - GPSIMD_TILES, M], F32, "low_vector", tag="after_bias_a")
+        low = [low_gpsimd[:, i, :] for i in range(GPSIMD_TILES)]
+        low.extend([low_vector[:, i, :] for i in range(ROW_TILES - GPSIMD_TILES)])
+
+        def times_load(i):
+            engine = nc.gpsimd if i < GPSIMD_TILES else nc.vector
+            engine.tensor_tensor(low[i], look_a[i][:], load_sb[i // PACK][:, i % PACK, :], ALU.mult)
+
+        def under_cap(i):
+            if i < GPSIMD_TILES:
+                nc.gpsimd.tensor_scalar(low[i], low[i], col("cap", i), FLOAT32_LOWEST, ALU.min, ALU.max)
+            else:
+                nc.vector.tensor_scalar(low[i], low[i], col("cap", i), None, ALU.min)
+
+        for first, last in ((0, GPSIMD_TILES - 1), (GPSIMD_TILES, ROW_TILES - 1)):
+            for i in range(first, last + 1):
+                times_load(i)
+                if i > first:
+                    under_cap(i - 1)
+            under_cap(last)
+
+        z = kept([P, M_HALVES, R_BLOCKS, PACK, MW], F32, "z", tag="after_exp")
+        y_bank = {
+            (u, k): psum.tile([P, BANK], F32, name="y_bank", tag="bank%d" % (u * PACK + k))
+            for u in range(M_HALVES)
+            for k in range(ROW_TILES // TILE_PAIR)
+        }
+
+        def y_acc(u, i):
+            return y_bank[u, i // TILE_PAIR][:, (i % TILE_PAIR) * MW : (i % TILE_PAIR + 1) * MW]
+
+        def round_to_words(dst, src):
             nc.vector.tensor_copy(
                 out=dst.rearrange("p (c i t) -> p c t i", i=PACK, t=PACK),
-                in_=src.rearrange("p (t c i) -> p c t i", i=PACK, t=PACK),
+                in_=src.rearrange("p t (c i) -> p c t i", i=PACK),
             )
 
-        for u in range(MH):
-            mcols = slice(u * MW, (u + 1) * MW)
-            yacc = [psum.tile([P, MW], F32, name="yacc", tag="bank%d" % j) for j in range(NG * PACK)]
-            for b in range(HB):
-                base = (u * HB + b) * PACK * MW
+        for u in range(M_HALVES):
+            m_cols = slice(u * MW, (u + 1) * MW)
+            for b in range(R_BLOCKS):
                 for t in range(PACK):
                     i = b * PACK + t
-                    zt = z[:, base + t * MW : base + (t + 1) * MW]
+                    z_t = z[:, u, b, t, :]
                     nc.scalar.activation(
-                        out=zt, in_=h[i][:].indirect(pos2_sb[:, u * MW // LIST : (u + 1) * MW // LIST]),
+                        out=z_t, in_=h[i][:].indirect(pos2_sb[:, u * MW // LIST : (u + 1) * MW // LIST]),
                         func=ACT.Sigmoid, bias=col("thr", i),
                     )
-                    nc.vector.scalar_tensor_tensor(zt, zt, col("lean", i), low[i][:, mcols], ALU.mult, ALU.add)
-                z_bf = stage.tile([P, PACK * MW], BF16, name="z_bf", align_bytes=64)
-                interleave(z_bf[:], z[:, base : base + PACK * MW])
-                nc.vector.quantize_mx(out=zq[u, b][:].bitcast(FP8X4), scales=zs[u, b][:], in_=z_bf[:])
-                for j in range(NG * PACK):
-                    c0 = b * N + j * P
+                    nc.vector.scalar_tensor_tensor(z_t, z_t, col("lean", i), low[i][:, m_cols], ALU.mult, ALU.add)
+                if (u, b) == (M_HALVES - 1, R_BLOCKS - 1):
+                    z_bf = kept([P, PACK * MW], BF16, "z_bf_last", tag="after_z")
+                else:
+                    z_bf = stage.tile([P, PACK * MW], BF16, name="z_bf", align_bytes=64)
+                round_to_words(z_bf[:], z[:, u, b])
+                z_q = kept([P, MW], U32, "z_q%d_%d" % (u, b))
+                z_s = kept([P, MW], U8, "z_s%d_%d" % (u, b))
+                nc.vector.quantize_mx(out=z_q[:].bitcast(FP8X4), scales=z_s[:], in_=z_bf[:])
+                for i in range(ROW_TILES):
+                    c0 = b * N + i * P
                     nc.tensor.matmul_mx(
-                        out=yacc[j][:],
-                        lhsT=w4w[:, 2 * c0 : 2 * (c0 + P)].bitcast(FP4X4),
-                        lhsT_scale=w4s[:, c0 : c0 + P],
-                        rhs=zq[u, b][:].bitcast(FP8X4),
-                        rhs_scale=zs[u, b][:],
-                        start=(b == 0),
-                        stop=(b == HB - 1),
+                        out=y_acc(u, i),
+                        lhsT=w4_w[:, 2 * c0 : 2 * (c0 + P)].bitcast(FP4X4),
+                        lhsT_scale=w4_s[:, c0 : c0 + P],
+                        rhs=z_q[:].bitcast(FP8X4),
+                        rhs_scale=z_s[:],
+                        start=(b == 0 and i % TILE_PAIR == 0),
+                        stop=(b == R_BLOCKS - 1 and i % TILE_PAIR == TILE_PAIR - 1),
                     )
-            for g in range(NG):
-                y = big.tile([P, PACK * MW], F32, name="y", tag="big", align_bytes=64)
+
+        y_s = kept([P, N_GROUPS * M], U8, "y_s")
+        y_bf_first = kept([P, N_GROUPS * PACK * MW], BF16, "y_bf_first", tag="after_z")
+        for u in range(M_HALVES):
+            m_cols = slice(u * MW, (u + 1) * MW)
+            for g in range(N_GROUPS):
+                y = big.tile([P, PACK, MW], F32, name="y", tag="big", align_bytes=64)
+                out_rows = out_0[g * PASS : (g + 1) * PASS, m_cols].rearrange("(p t) m -> p t m", t=PACK)
                 for t in range(PACK):
-                    j = g * PACK + t
-                    yt = y[:, t * MW : (t + 1) * MW]
-                    if u == MH - 1 and t % 2 == 1:
-                        nc.vector.tensor_scalar(yt, yacc[j][:], col("rate", j), None, ALU.mult)
-                    else:
-                        nc.scalar.activation(out=yt, in_=yacc[j][:], func=ACT.Copy, scale=col("rate", j))
-                nc.sync.dma_start(
-                    out=out_0[g * PASS : (g + 1) * PASS, mcols].rearrange("(p t) m -> p t m", t=PACK),
-                    in_=y[:].rearrange("p (t m) -> p t m", t=PACK),
-                )
-                y_bf = stage.tile([P, PACK * MW], BF16, name="y_bf", align_bytes=64)
-                interleave(y_bf[:], y[:])
+                    i = g * PACK + t
+                    nc.scalar.activation(out=y[:, t, :], in_=y_acc(u, i), func=ACT.Copy, scale=col("rate", i))
+                    if t % TILE_PAIR == TILE_PAIR - 1:
+                        pair = slice(t + 1 - TILE_PAIR, t + 1)
+                        nc.sync.dma_start(out=out_rows[:, pair], in_=y[:, pair])
+                if u == 0:
+                    y_bf = y_bf_first[:, g * PACK * MW : (g + 1) * PACK * MW]
+                else:
+                    y_bf = stage.tile([P, PACK * MW], BF16, name="y_bf", align_bytes=64)[:]
+                round_to_words(y_bf, y[:])
+                y_q = kept([P, MW], U32, "y_q%d_%d" % (u, g))
                 nc.vector.quantize_mx(
-                    out=yq[u, g][:].bitcast(FP8X4), scales=ys[:, g * M + u * MW : g * M + (u + 1) * MW], in_=y_bf[:]
+                    out=y_q[:].bitcast(FP8X4), scales=y_s[:, g * M + u * MW : g * M + (u + 1) * MW], in_=y_bf
                 )
                 nc.sync.dma_start(
-                    out=out_1[g].rearrange("p m t -> p (m t)").bitcast(I32)[:, mcols], in_=yq[u, g][:].bitcast(I32)
+                    out=out_1[g].rearrange("p m t -> p (m t)").bitcast(I32)[:, m_cols], in_=y_q[:].bitcast(I32)
                 )
-        for q in range(4):
+        for q in range(QUADS):
             nc.scalar.dma_start(
-                out=out_2[:, 4 * q : 4 * q + 4, :].rearrange("g r m -> r g m").bitcast(I32),
-                in_=ys[32 * q : 32 * q + 4, :].bitcast(I32).rearrange("p (g m) -> p g m", g=NG),
+                out=out_2[:, PACK * q : PACK * (q + 1), :].rearrange("g r m -> r g m").bitcast(I32),
+                in_=y_s[QUAD * q : QUAD * q + PACK, :].bitcast(I32).rearrange("p (g m) -> p g m", g=N_GROUPS),
             )

from contextlib import ExitStack

import concourse.mybir as mybir

K, T, S, H, N, M = 1536, 2048, 1024, 1024, 1024, 512
FLOPS = 2 * K * H * S + 2 * H * N * M

F32 = mybir.dt.float32
BF16 = mybir.dt.bfloat16
I32 = mybir.dt.int32
U32 = mybir.dt.uint32
U16 = mybir.dt.uint16
U8 = mybir.dt.uint8
FP8X4 = mybir.dt.float8_e4m3fn_x4
FP4X4 = mybir.dt.float4_e2m1fn_x4
ALU = mybir.AluOpType
ACT = mybir.ActivationFunctionType

P = 128
PACK = 4
PASS = P * PACK
QUADS, QUAD = 4, 32
BANK = 512
LIST = 16
K_PASSES = K // PASS
R_BLOCKS = H // PASS
N_GROUPS = N // PASS
ROW_TILES = R_BLOCKS * PACK
S_HALVES = S // BANK
M_HALVES = 2
MW = M // M_HALVES
TILE_PAIR = PACK // 2
GPSIMD_TILES = 3
FLOAT32_LOWEST = -3.4028234663852886e38


def tile_list_covenant_watch_looks_kernel(
    tc, tab_words, tab_scales, offs, pos1, pos2, w1, temp, thr, load, cap, lean, w4_words, w4_scales, rate, out_0, out_1, out_2
):
    nc = tc.nc
    with ExitStack() as ctx:
        keep = ctx.enter_context(tc.tile_pool(name="keep", bufs=1))
        big = ctx.enter_context(tc.tile_pool(name="big", bufs=5))
        stage = ctx.enter_context(tc.tile_pool(name="stage", bufs=2))
        psum = ctx.enter_context(tc.psum_pool(name="psum", bufs=1))

        def kept(shape, dtype, name, tag=None):
            return keep.tile(shape, dtype, name=name, tag=tag or name, align_bytes=64)

        offs_sb = kept([P, S // LIST], U16, "offs_sb")
        pos1_sb = kept([P, M // LIST], U16, "pos1_sb")
        pos2_sb = kept([P, M // LIST], U16, "pos2_sb")
        tab_w = [kept([P, T], U32, "tab_w%d" % a) for a in range(K_PASSES)]
        tab_s = kept([P, T], U8, "tab_s")
        w4_w_raw = kept([P, R_BLOCKS, 2 * N], U8, "w4_w_raw")
        w4_s_raw = kept([P, R_BLOCKS, N], U8, "w4_s_raw")
        load_sb = [kept([P, PACK, M], F32, "load_sb%d" % b) for b in range(R_BLOCKS)]
        w1_raw = {}
        row_vec = {}

        def load_tab_words(a):
            nc.sync.dma_start(out=tab_w[a][:].bitcast(I32), in_=tab_words[a].rearrange("p t i -> p (t i)").bitcast(I32))

        def load_w1(b, a):
            w1_raw[b, a] = big.tile([P, PACK, PASS], F32, name="w1_raw", tag="big", align_bytes=64)
            rows = w1[a * PASS : (a + 1) * PASS, b * PASS : (b + 1) * PASS]
            nc.sync.dma_start(out=w1_raw[b, a][:], in_=rows.rearrange("(p j) c -> p j c", j=PACK))

        def load_row_vec(name, vec):
            row_vec[name] = kept([P, ROW_TILES], F32, name + "_sb")
            nc.sync.dma_start(
                out=row_vec[name][:].rearrange("p (b t) -> p b t", t=PACK),
                in_=vec.rearrange("(b p t) -> p b t", p=P, t=PACK),
            )

        def col(name, i):
            return row_vec[name][:, i : i + 1]

        nc.vector.memset(tab_s[:].bitcast(I32), 0)
        nc.gpsimd.memset(w4_s_raw[:].bitcast(I32), 0)

        load_tab_words(0)
        nc.sync.dma_start(offs_sb[:], offs)
        load_tab_words(1)
        for q in range(QUADS):
            nc.sync.dma_start(
                out=tab_s[QUAD * q : QUAD * q + PACK * K_PASSES, :].bitcast(I32),
                in_=tab_scales[:, PACK * q : PACK * (q + 1), :].bitcast(I32),
            )
        load_w1(0, 0)
        load_w1(0, 1)
        for q in range(QUADS):
            nc.sync.dma_start(
                out=w4_s_raw[QUAD * q : QUAD * q + PACK, :, :].bitcast(I32),
                in_=w4_scales[:, PACK * q : PACK * (q + 1), :].rearrange("a r c -> r a c").bitcast(I32),
            )
        load_tab_words(2)
        load_row_vec("temp", temp)
        load_w1(0, 2)
        nc.sync.dma_start(pos1_sb[:], pos1)
        for a in range(K_PASSES):
            load_w1(1, a)
        load_row_vec("cap", cap)
        for b in range(R_BLOCKS):
            rows = load[b * PASS : (b + 1) * PASS, :]
            nc.sync.dma_start(out=load_sb[b][:], in_=rows.rearrange("(p t) m -> p t m", t=PACK))
        nc.sync.dma_start(out=w4_w_raw[:].bitcast(I32), in_=w4_words.rearrange("a p c -> p a c").bitcast(I32))
        nc.sync.dma_start(pos2_sb[:], pos2)
        for name, vec in (("thr", thr), ("lean", lean), ("rate", rate)):
            load_row_vec(name, vec)

        v_w = {(a, s): kept([P, BANK], U32, "v_w%d_%d" % (a, s)) for a in range(K_PASSES) for s in range(S_HALVES)}
        v_s = [kept([P, BANK], U8, "v_s%d" % s) for s in range(S_HALVES)]
        w1_q = {(b, a): kept([P, PASS], U32, "w1_q%d_%d" % (b, a)) for b in range(R_BLOCKS) for a in range(K_PASSES)}
        w1_s = {(b, a): kept([P, PASS], U8, "w1_s%d_%d" % (b, a)) for b in range(R_BLOCKS) for a in range(K_PASSES)}
        h_acc = {}

        def offs_half(s):
            return offs_sb[:, s * BANK // LIST : (s + 1) * BANK // LIST]

        def gather_words(a):
            for s in range(S_HALVES):
                nc.vector.tensor_copy(v_w[a, s][:], tab_w[a][:].indirect(offs_half(s)))

        def gather_scales():
            for s in range(S_HALVES):
                nc.vector.tensor_copy(v_s[s][:], tab_s[:].indirect(offs_half(s)))

        def quantise_w1(b, a):
            if (b, a) == (R_BLOCKS - 1, K_PASSES - 1):
                w1_bf = kept([P, PASS * PACK], BF16, "w1_bf_last", tag="after_w1")
            else:
                w1_bf = stage.tile([P, PASS * PACK], BF16, name="w1_bf", bufs=3, align_bytes=64)
            dst = w1_bf[:].rearrange("p (t q j) -> p q j t", t=PACK, j=PACK)
            src = w1_raw[b, a][:].rearrange("p j (q t) -> p q j t", t=PACK)
            if a == K_PASSES - 1:
                shares = ((nc.vector.tensor_copy, 0, TILE_PAIR), (nc.scalar.copy, TILE_PAIR, PACK))
            else:
                shares = ((nc.scalar.copy, 0, PACK),)
            for copy, t0, t1 in shares:
                copy(out=dst[:, :, :, t0:t1], in_=src[:, :, :, t0:t1])
                cols = slice(t0 * P, t1 * P)
                nc.vector.quantize_mx(
                    out=w1_q[b, a][:, cols].bitcast(FP8X4),
                    scales=w1_s[b, a][:, cols],
                    in_=w1_bf[:, t0 * PASS : t1 * PASS],
                )

        def first_product(b, t):
            cols = slice(t * P, (t + 1) * P)
            for a in range(K_PASSES):
                for s in range(S_HALVES):
                    if a == 0:
                        h_acc[b * PACK + t, s] = psum.tile([P, BANK], F32, name="h_acc", tag="bank%d" % (t * S_HALVES + s))
                    nc.tensor.matmul_mx(
                        out=h_acc[b * PACK + t, s][:],
                        lhsT=w1_q[b, a][:, cols].bitcast(FP8X4),
                        lhsT_scale=w1_s[b, a][:, cols],
                        rhs=v_w[a, s][:].bitcast(FP8X4),
                        rhs_scale=v_s[s][PACK * a :, :],
                        start=(a == 0),
                        stop=(a == K_PASSES - 1),
                    )

        neg_temp = kept([P, ROW_TILES], F32, "neg_temp", tag="after_bias_a")
        half_top = kept([P, S_HALVES, ROW_TILES], F32, "half_top", tag="after_bias_b")
        exp_bias = kept([P, ROW_TILES], F32, "exp_bias", tag="after_exp")
        h = [kept([P, S], F32, "h%d" % i) for i in range(ROW_TILES)]
        look_a = [kept([P, M], F32, "look_a%d" % i) for i in range(ROW_TILES)]

        def leave_psum(i):
            for s in range(S_HALVES):
                nc.vector.tensor_scalar(
                    h[i][:, s * BANK : (s + 1) * BANK], h_acc[i, s][:], 1.0, None, ALU.mult, ALU.max,
                    accum_out=half_top[:, s, i : i + 1],
                )
            nc.vector.tensor_scalar(
                exp_bias[:, i : i + 1], half_top[:, 0, i : i + 1], half_top[:, 1, i : i + 1], neg_temp[:, i : i + 1],
                ALU.max, ALU.mult,
            )

        def look_exp(i):
            nc.scalar.activation(
                out=look_a[i][:], in_=h[i][:].indirect(pos1_sb[:]), func=ACT.Exp,
                bias=exp_bias[:, i : i + 1], scale=col("temp", i),
            )

        for a in range(K_PASSES - 1):
            gather_words(a)
        gather_scales()
        for a in range(K_PASSES - 1):
            quantise_w1(0, a)
        gather_words(K_PASSES - 1)
        quantise_w1(0, K_PASSES - 1)
        nc.vector.tensor_scalar(neg_temp[:], row_vec["temp"][:], -1.0, None, ALU.mult)
        w4_s = kept([P, R_BLOCKS * N], U8, "w4_s")
        nc.vector.tensor_copy(
            out=w4_s[:].rearrange("p (g t q) -> p g t q", t=PACK, q=P),
            in_=w4_s_raw[:].rearrange("p a (g q t) -> p (a g) t q", t=PACK, q=P),
        )
        for t in range(PACK):
            first_product(0, t)
        for a in range(K_PASSES):
            quantise_w1(1, a)
        for t in range(PACK):
            leave_psum(t)
        for t in range(PACK):
            look_exp(t)
        for t in range(PACK):
            first_product(1, t)
        for t in range(PACK):
            leave_psum(PACK + t)
            look_exp(PACK + t)

        w4_w = kept([P, R_BLOCKS * 2 * N], U8, "w4_w", tag="after_bias_b")
        nc.vector.tensor_copy(
            out=w4_w[:].bitcast(U16).rearrange("p (g t q) -> p g t q", t=PACK, q=P),
            in_=w4_w_raw[:].bitcast(U16).rearrange("p a (g q t) -> p (a g) t q", t=PACK, q=P),
        )

        low_gpsimd = kept([P, GPSIMD_TILES, M], F32, "low_gpsimd", tag="after_w1")
        low_vector = kept([P, ROW_TILES - GPSIMD_TILES, M], F32, "low_vector", tag="after_bias_a")
        low = [low_gpsimd[:, i, :] for i in range(GPSIMD_TILES)]
        low.extend([low_vector[:, i, :] for i in range(ROW_TILES - GPSIMD_TILES)])

        def times_load(i):
            engine = nc.gpsimd if i < GPSIMD_TILES else nc.vector
            engine.tensor_tensor(low[i], look_a[i][:], load_sb[i // PACK][:, i % PACK, :], ALU.mult)

        def under_cap(i):
            if i < GPSIMD_TILES:
                nc.gpsimd.tensor_scalar(low[i], low[i], col("cap", i), FLOAT32_LOWEST, ALU.min, ALU.max)
            else:
                nc.vector.tensor_scalar(low[i], low[i], col("cap", i), None, ALU.min)

        for first, last in ((0, GPSIMD_TILES - 1), (GPSIMD_TILES, ROW_TILES - 1)):
            for i in range(first, last + 1):
                times_load(i)
                if i > first:
                    under_cap(i - 1)
            under_cap(last)

        z = kept([P, M_HALVES, R_BLOCKS, PACK, MW], F32, "z", tag="after_exp")
        y_bank = {
            (u, k): psum.tile([P, BANK], F32, name="y_bank", tag="bank%d" % (u * PACK + k))
            for u in range(M_HALVES)
            for k in range(ROW_TILES // TILE_PAIR)
        }

        def y_acc(u, i):
            return y_bank[u, i // TILE_PAIR][:, (i % TILE_PAIR) * MW : (i % TILE_PAIR + 1) * MW]

        def round_to_words(dst, src):
            nc.vector.tensor_copy(
                out=dst.rearrange("p (c i t) -> p c t i", i=PACK, t=PACK),
                in_=src.rearrange("p t (c i) -> p c t i", i=PACK),
            )

        for u in range(M_HALVES):
            m_cols = slice(u * MW, (u + 1) * MW)
            for b in range(R_BLOCKS):
                for t in range(PACK):
                    i = b * PACK + t
                    z_t = z[:, u, b, t, :]
                    nc.scalar.activation(
                        out=z_t, in_=h[i][:].indirect(pos2_sb[:, u * MW // LIST : (u + 1) * MW // LIST]),
                        func=ACT.Sigmoid, bias=col("thr", i),
                    )
                    nc.vector.scalar_tensor_tensor(z_t, z_t, col("lean", i), low[i][:, m_cols], ALU.mult, ALU.add)
                if (u, b) == (M_HALVES - 1, R_BLOCKS - 1):
                    z_bf = kept([P, PACK * MW], BF16, "z_bf_last", tag="after_z")
                else:
                    z_bf = stage.tile([P, PACK * MW], BF16, name="z_bf", align_bytes=64)
                round_to_words(z_bf[:], z[:, u, b])
                z_q = kept([P, MW], U32, "z_q%d_%d" % (u, b))
                z_s = kept([P, MW], U8, "z_s%d_%d" % (u, b))
                nc.vector.quantize_mx(out=z_q[:].bitcast(FP8X4), scales=z_s[:], in_=z_bf[:])
                for i in range(ROW_TILES):
                    c0 = b * N + i * P
                    nc.tensor.matmul_mx(
                        out=y_acc(u, i),
                        lhsT=w4_w[:, 2 * c0 : 2 * (c0 + P)].bitcast(FP4X4),
                        lhsT_scale=w4_s[:, c0 : c0 + P],
                        rhs=z_q[:].bitcast(FP8X4),
                        rhs_scale=z_s[:],
                        start=(b == 0 and i % TILE_PAIR == 0),
                        stop=(b == R_BLOCKS - 1 and i % TILE_PAIR == TILE_PAIR - 1),
                    )

        y_s = kept([P, N_GROUPS * M], U8, "y_s")
        y_bf_first = kept([P, N_GROUPS * PACK * MW], BF16, "y_bf_first", tag="after_z")
        for u in range(M_HALVES):
            m_cols = slice(u * MW, (u + 1) * MW)
            for g in range(N_GROUPS):
                y = big.tile([P, PACK, MW], F32, name="y", tag="big", align_bytes=64)
                out_rows = out_0[g * PASS : (g + 1) * PASS, m_cols].rearrange("(p t) m -> p t m", t=PACK)
                for t in range(PACK):
                    i = g * PACK + t
                    nc.scalar.activation(out=y[:, t, :], in_=y_acc(u, i), func=ACT.Copy, scale=col("rate", i))
                    if t % TILE_PAIR == TILE_PAIR - 1:
                        pair = slice(t + 1 - TILE_PAIR, t + 1)
                        nc.sync.dma_start(out=out_rows[:, pair], in_=y[:, pair])
                if u == 0:
                    y_bf = y_bf_first[:, g * PACK * MW : (g + 1) * PACK * MW]
                else:
                    y_bf = stage.tile([P, PACK * MW], BF16, name="y_bf", align_bytes=64)[:]
                round_to_words(y_bf, y[:])
                y_q = kept([P, MW], U32, "y_q%d_%d" % (u, g))
                nc.vector.quantize_mx(
                    out=y_q[:].bitcast(FP8X4), scales=y_s[:, g * M + u * MW : g * M + (u + 1) * MW], in_=y_bf
                )
                nc.sync.dma_start(
                    out=out_1[g].rearrange("p m t -> p (m t)").bitcast(I32)[:, m_cols], in_=y_q[:].bitcast(I32)
                )
        for q in range(QUADS):
            nc.scalar.dma_start(
                out=out_2[:, PACK * q : PACK * (q + 1), :].rearrange("g r m -> r g m").bitcast(I32),
                in_=y_s[QUAD * q : QUAD * q + PACK, :].bitcast(I32).rearrange("p (g m) -> p g m", g=N_GROUPS),
            )
